import numpy as np
import ml_dtypes

BF16 = ml_dtypes.bfloat16


def bf(x):
    return np.asarray(x, np.float32).astype(BF16)


def f32(x):
    return np.asarray(x, np.float32)


def f64(x):
    return np.asarray(x).astype(np.float64)


def striped(idx):
    return np.tile(idx.reshape(-1, 16).T, (8, 1))


S, K, M, N, V, D = 256, 128, 128, 192, 8, 32


def setup_inputs():
    return {"base": bf(np.random.standard_normal((M, S))), "x": bf(np.random.standard_normal((K, N))), "w": bf(1.5 * np.random.standard_normal((K, M)) / np.sqrt(K)), "s": f32(0.5 + np.random.random_sample((M, 1))), "offs": striped(np.random.permutation(S)[:N])}


def reference(base, x, w, s, offs):
    idx = offs[:16].T.reshape(-1)
    z = f64(base).copy()
    z[:, idx] += f64(w).T @ f64(x)
    z = z * f64(s)
    u = z.reshape(M, V, D)
    u = u - u.max(axis=2, keepdims=True)
    u = np.exp(u)
    u = u / u.sum(axis=2, keepdims=True)
    return u.reshape(M, S)

@@ -1,0 +1,59 @@
+import concourse.mybir as mybir
+from concourse.masks import make_identity
+
+BF16, F32, U16 = mybir.dt.bfloat16, mybir.dt.float32, mybir.dt.uint16
+ALU = mybir.AluOpType
+EXP = mybir.ActivationFunctionType.Exp
+X_AXIS = mybir.AxisListType.X
+
+P = 128
+WORDS, PICKED = 256, 192
+SLATES, SLATE = 8, 32
+
+FLOPS = 2 * P * P * PICKED + 5 * P * WORDS
+
+
+def tile_rows_rescore_kernel(tc, base, x, w, s, offs, out):
+    nc = tc.nc
+    with (
+        tc.tile_pool(name="held", bufs=1) as held,
+        tc.psum_pool(name="psum", bufs=1) as psum,
+    ):
+        base_t = held.tile([P, WORDS], BF16, name="base_t")
+        offsets = held.tile([P, PICKED // 16], U16, name="offsets")
+        w_t = held.tile([P, P], BF16, name="w_t")
+        x_t = held.tile([P, PICKED], BF16, name="x_t")
+        s_t = held.tile([P, 1], F32, name="s_t")
+        nc.sync.dma_start(base_t[:], base)
+        nc.sync.dma_start(offsets[:], offs)
+        nc.scalar.dma_start(w_t[:], w)
+        nc.scalar.dma_start(x_t[:], x)
+        nc.scalar.dma_start(s_t[:], s)
+
+        ident = held.tile([P, P], BF16, name="ident")
+        make_identity(nc, ident[:])
+
+        warm = held.tile([P, 1], F32, name="warm")
+        nc.vector.memset(warm[:], 0.0)
+        warm_exp = held.tile([P, 1], F32, name="warm_exp")
+        nc.scalar.activation(warm_exp[:], warm[:], EXP)
+
+        z = psum.tile([P, WORDS], F32, name="z")
+        nc.tensor.matmul(z[:], ident[:], base_t[:], start=True, stop=False)
+        nc.tensor.matmul(z[:].indirect(offsets[:]), w_t[:], x_t[:], start=False, stop=True)
+
+        t = held.tile([P, SLATES, SLATE], F32, name="t")
+        nc.vector.tensor_scalar(t[:].rearrange("p v d -> p (v d)"), z[:], s_t[:], None, op0=ALU.mult)
+        top = held.tile([P, SLATES], F32, name="top")
+        nc.vector.reduce_max(top[:], t[:], axis=X_AXIS)
+        shifted = held.tile([P, SLATES, SLATE], F32, name="shifted")
+        nc.vector.tensor_tensor(shifted[:], t[:], top[:].unsqueeze(2).to_broadcast([P, SLATES, SLATE]), ALU.subtract)
+        e = held.tile([P, SLATES, SLATE], F32, name="e")
+        nc.scalar.activation(e[:], shifted[:], EXP)
+        total = held.tile([P, SLATES], F32, name="total")
+        nc.vector.reduce_sum(total[:], e[:], axis=X_AXIS)
+        share = held.tile([P, SLATES], F32, name="share")
+        nc.vector.reciprocal(share[:], total[:])
+        result = held.tile([P, SLATES, SLATE], F32, name="result")
+        nc.vector.tensor_tensor(result[:], e[:], share[:].unsqueeze(2).to_broadcast([P, SLATES, SLATE]), ALU.mult)
+        nc.sync.dma_start(out, result[:].rearrange("p v d -> p (v d)"))

@@ -43,17 +43,23 @@ def tile_rows_rescore_kernel(tc, base, x, w, s, offs, out):
         nc.tensor.matmul(z[:].indirect(offsets[:]), w_t[:], x_t[:], start=False, stop=True)
 
         t = held.tile([P, SLATES, SLATE], F32, name="t")
-        nc.vector.tensor_scalar(t[:].rearrange("p v d -> p (v d)"), z[:], s_t[:], None, op0=ALU.mult)
-        top = held.tile([P, SLATES], F32, name="top")
-        nc.vector.reduce_max(top[:], t[:], axis=X_AXIS)
-        shifted = held.tile([P, SLATES, SLATE], F32, name="shifted")
-        nc.vector.tensor_tensor(shifted[:], t[:], top[:].unsqueeze(2).to_broadcast([P, SLATES, SLATE]), ALU.subtract)
+        low = held.tile([P, SLATES], F32, name="low")
         e = held.tile([P, SLATES, SLATE], F32, name="e")
-        nc.scalar.activation(e[:], shifted[:], EXP)
         total = held.tile([P, SLATES], F32, name="total")
-        nc.vector.reduce_sum(total[:], e[:], axis=X_AXIS)
         share = held.tile([P, SLATES], F32, name="share")
-        nc.vector.reciprocal(share[:], total[:])
         result = held.tile([P, SLATES, SLATE], F32, name="result")
-        nc.vector.tensor_tensor(result[:], e[:], share[:].unsqueeze(2).to_broadcast([P, SLATES, SLATE]), ALU.mult)
+        nc.vector.tensor_scalar(t[:].rearrange("p v d -> p (v d)"), z[:], s_t[:], None, op0=ALU.mult)
+        HALF = SLATES // 2
+        for v0 in (0, HALF):
+            half = slice(v0, v0 + HALF)
+            nc.vector.tensor_reduce(low[:, half], t[:, half, :], axis=X_AXIS, op=ALU.max, negate=True)
+            for v in range(v0, v0 + HALF):
+                nc.scalar.activation(e[:, v, :], t[:, v, :], EXP, bias=low[:, v : v + 1])
+        for v0 in (0, HALF):
+            half = slice(v0, v0 + HALF)
+            nc.vector.reduce_sum(total[:, half], e[:, half, :], axis=X_AXIS)
+            nc.vector.reciprocal(share[:, half], total[:, half])
+            nc.vector.tensor_tensor(
+                result[:, half, :], e[:, half, :], share[:, half].unsqueeze(2).to_broadcast([P, HALF, SLATE]), ALU.mult
+            )
         nc.sync.dma_start(out, result[:].rearrange("p v d -> p (v d)"))

@@ -48,18 +48,20 @@ def tile_rows_rescore_kernel(tc, base, x, w, s, offs, out):
         total = held.tile([P, SLATES], F32, name="total")
         share = held.tile([P, SLATES], F32, name="share")
         result = held.tile([P, SLATES, SLATE], F32, name="result")
-        nc.vector.tensor_scalar(t[:].rearrange("p v d -> p (v d)"), z[:], s_t[:], None, op0=ALU.mult)
-        HALF = SLATES // 2
-        for v0 in (0, HALF):
-            half = slice(v0, v0 + HALF)
-            nc.vector.tensor_reduce(low[:, half], t[:, half, :], axis=X_AXIS, op=ALU.max, negate=True)
-            for v in range(v0, v0 + HALF):
-                nc.scalar.activation(e[:, v, :], t[:, v, :], EXP, bias=low[:, v : v + 1])
-        for v0 in (0, HALF):
-            half = slice(v0, v0 + HALF)
-            nc.vector.reduce_sum(total[:, half], e[:, half, :], axis=X_AXIS)
-            nc.vector.reciprocal(share[:, half], total[:, half])
+        PAIR = 2
+        pairs = [slice(v, v + PAIR) for v in range(0, SLATES, PAIR)]
+        for pair in pairs:
+            nc.vector.tensor_scalar(
+                t[:, pair, :].rearrange("p v d -> p (v d)"), z[:, pair.start * SLATE : pair.stop * SLATE], s_t[:], None, op0=ALU.mult
+            )
+        for pair in pairs:
+            nc.vector.tensor_reduce(low[:, pair], t[:, pair, :], axis=X_AXIS, op=ALU.max, negate=True)
+            for v in range(pair.start, pair.stop):
+                nc.scalar.activation(e[:, v, :], t[:, v, :], EXP, bias=low[:, v : v + 1], accum_out=total[:, v : v + 1])
+        for pair in pairs:
+            nc.vector.reciprocal(share[:, pair], total[:, pair])
+        for pair in pairs:
             nc.vector.tensor_tensor(
-                result[:, half, :], e[:, half, :], share[:, half].unsqueeze(2).to_broadcast([P, HALF, SLATE]), ALU.mult
+                result[:, pair, :], e[:, pair, :], share[:, pair].unsqueeze(2).to_broadcast([P, PAIR, SLATE]), ALU.mult
             )
         nc.sync.dma_start(out, result[:].rearrange("p v d -> p (v d)"))

@@ -26,9 +26,9 @@ def tile_rows_rescore_kernel(tc, base, x, w, s, offs, out):
         s_t = held.tile([P, 1], F32, name="s_t")
         nc.sync.dma_start(base_t[:], base)
         nc.sync.dma_start(offsets[:], offs)
-        nc.scalar.dma_start(w_t[:], w)
-        nc.scalar.dma_start(x_t[:], x)
-        nc.scalar.dma_start(s_t[:], s)
+        nc.sync.dma_start(w_t[:], w)
+        nc.sync.dma_start(x_t[:], x)
+        nc.sync.dma_start(s_t[:], s)
 
         ident = held.tile([P, P], BF16, name="ident")
         make_identity(nc, ident[:])

import concourse.mybir as mybir
from concourse.masks import make_identity

BF16, F32, U16 = mybir.dt.bfloat16, mybir.dt.float32, mybir.dt.uint16
ALU = mybir.AluOpType
EXP = mybir.ActivationFunctionType.Exp
X_AXIS = mybir.AxisListType.X

P = 128
WORDS, PICKED = 256, 192
SLATES, SLATE = 8, 32

FLOPS = 2 * P * P * PICKED + 5 * P * WORDS


def tile_rows_rescore_kernel(tc, base, x, w, s, offs, out):
    nc = tc.nc
    with (
        tc.tile_pool(name="held", bufs=1) as held,
        tc.psum_pool(name="psum", bufs=1) as psum,
    ):
        base_t = held.tile([P, WORDS], BF16, name="base_t")
        offsets = held.tile([P, PICKED // 16], U16, name="offsets")
        w_t = held.tile([P, P], BF16, name="w_t")
        x_t = held.tile([P, PICKED], BF16, name="x_t")
        s_t = held.tile([P, 1], F32, name="s_t")
        nc.sync.dma_start(base_t[:], base)
        nc.sync.dma_start(offsets[:], offs)
        nc.sync.dma_start(w_t[:], w)
        nc.sync.dma_start(x_t[:], x)
        nc.sync.dma_start(s_t[:], s)

        ident = held.tile([P, P], BF16, name="ident")
        make_identity(nc, ident[:])

        warm = held.tile([P, 1], F32, name="warm")
        nc.vector.memset(warm[:], 0.0)
        warm_exp = held.tile([P, 1], F32, name="warm_exp")
        nc.scalar.activation(warm_exp[:], warm[:], EXP)

        z = psum.tile([P, WORDS], F32, name="z")
        nc.tensor.matmul(z[:], ident[:], base_t[:], start=True, stop=False)
        nc.tensor.matmul(z[:].indirect(offsets[:]), w_t[:], x_t[:], start=False, stop=True)

        t = held.tile([P, SLATES, SLATE], F32, name="t")
        low = held.tile([P, SLATES], F32, name="low")
        e = held.tile([P, SLATES, SLATE], F32, name="e")
        total = held.tile([P, SLATES], F32, name="total")
        share = held.tile([P, SLATES], F32, name="share")
        result = held.tile([P, SLATES, SLATE], F32, name="result")
        PAIR = 2
        pairs = [slice(v, v + PAIR) for v in range(0, SLATES, PAIR)]
        for pair in pairs:
            nc.vector.tensor_scalar(
                t[:, pair, :].rearrange("p v d -> p (v d)"), z[:, pair.start * SLATE : pair.stop * SLATE], s_t[:], None, op0=ALU.mult
            )
        for pair in pairs:
            nc.vector.tensor_reduce(low[:, pair], t[:, pair, :], axis=X_AXIS, op=ALU.max, negate=True)
            for v in range(pair.start, pair.stop):
                nc.scalar.activation(e[:, v, :], t[:, v, :], EXP, bias=low[:, v : v + 1], accum_out=total[:, v : v + 1])
        for pair in pairs:
            nc.vector.reciprocal(share[:, pair], total[:, pair])
        for pair in pairs:
            nc.vector.tensor_tensor(
                result[:, pair, :], e[:, pair, :], share[:, pair].unsqueeze(2).to_broadcast([P, PAIR, SLATE]), ALU.mult
            )
        nc.sync.dma_start(out, result[:].rearrange("p v d -> p (v d)"))
